import numpy as np
import ml_dtypes


def mxq(x, axis, fmt="e4m3"):
    dtype, down = {"e4m3": (ml_dtypes.float8_e4m3fn, 7), "e5m2": (ml_dtypes.float8_e5m2, 14)}[fmt]
    v = np.moveaxis(np.asarray(x, np.float32).astype(ml_dtypes.bfloat16).astype(np.float64), axis, -1)
    blocks = v.reshape(v.shape[:-1] + (-1, 32))
    amax = np.abs(blocks).max(-1, keepdims=True)
    byte = np.maximum(np.where(amax > 0, np.frexp(amax)[1] - 1 + 127, 0) - down, 1)
    scale = np.exp2(byte - 127.0)
    codes = (blocks / scale).astype(np.float32).astype(dtype).astype(np.float64)
    return np.moveaxis((codes * scale).reshape(v.shape), -1, axis)


WIDE = False


def mx_kscale(k):
    if not WIDE:
        return np.ones(k)
    levels = np.array([10, -10, 5, -5, 0])
    if k % 512:
        return np.exp2(np.random.permutation(np.resize(levels, k // 32))).repeat(32)
    a = np.empty((k // 512, 16))
    for p in range(k // 512):
        a[p, :8] = np.random.permutation(np.resize(levels, 8))
        for g in range(8):
            far = levels[np.abs(levels - a[p, g]) >= 10]
            a[p, g + 8] = far[np.random.randint(len(far))]
    return np.exp2(a.ravel()).repeat(32)


def f64(x):
    return np.asarray(x).astype(np.float64)


def striped(idx):
    return np.tile(idx.reshape(-1, 16).T, (8, 1)).astype(np.uint16)


def unstriped(offs):
    return offs[:16].T.reshape(-1).astype(np.int64)


def pack_weight(w):
    k, n = w.shape
    w = f64(np.asarray(w, np.float32).astype(ml_dtypes.bfloat16)).reshape(k // 32, 32, n)
    amax = np.abs(w).max(1)
    byte = np.clip(np.where(amax > 0, np.frexp(amax)[1] - 1 + 127 - 7, 1), 1, 254)
    scaled = (w * np.exp2(127.0 - byte)[:, None, :]).reshape(k, n).astype(np.float32)
    words = np.ascontiguousarray(scaled.reshape(k // 512, 128, 4, n).transpose(0, 1, 3, 2)).astype(ml_dtypes.float8_e4m3fn).view(np.uint8)
    return words, np.ascontiguousarray(byte.astype(np.uint8).reshape(k // 512, 16, n))


def unpack_weight(words, scales):
    g, p, n, _ = words.shape
    vals = np.ascontiguousarray(words).view(ml_dtypes.float8_e4m3fn).astype(np.float64) * np.repeat(np.exp2(scales.astype(np.float64) - 127.0), 8, axis=1)[..., None]
    return vals.transpose(0, 1, 3, 2).reshape(g * 512, n)


def relu(v):
    return np.maximum(v, 0.0)


K, T, S, N, H = 1024, 2048, 512, 128, 512


def setup_inputs():
    n = np.random.standard_normal
    s = mx_kscale(K)[:, None]
    u = mx_kscale(H)
    packed_xT = pack_weight(n((K, T)) * s)
    return {
        "x_words": packed_xT[0],
        "x_scales": packed_xT[1],
        "w1": (n((K, H)) / np.sqrt(K) / s).astype(np.float32),
        "w2": (n((K, H)) / np.sqrt(K) / s).astype(np.float32),
        "pen": (np.random.uniform(1.0, 2.0, (H, 1))).astype(np.float32),
        "unit": (np.random.uniform(0.6, 1.4, (H, 1)) * u[:, None]).astype(np.float32),
        "w3": (n((H, N)) / np.sqrt(H) / u[:, None]).astype(np.float32),
        "offs": striped(np.random.permutation(T)[:S]),
        "nb1": striped(np.random.permutation(S)),
        "nb2": striped(np.random.permutation(S)),
    }


def reference(x_words, x_scales, w1, w2, pen, unit, w3, offs, nb1, nb2):
    xq = unpack_weight(x_words, x_scales)[:, unstriped(offs)]
    dm = mxq(f64(w1), 0, "e4m3").T @ xq
    dem = np.log(np.exp(dm) + 1.0)
    st = mxq(f64(w2), 0, "e4m3").T @ xq
    stk = np.log(np.exp(st) + 1.0)
    shrt = relu(dem - stk)
    exc = relu(stk - dem)
    e1 = exc[:, unstriped(nb1)]
    tr1 = np.minimum(shrt, e1)
    shrt2 = shrt - tr1
    e2 = exc[:, unstriped(nb2)]
    tr2 = np.minimum(shrt2, 0.5 * e2)
    lost = shrt2 - tr2
    cost = f64(pen) * lost + 0.3 * exc + 0.5 * (tr1 + tr2)
    hid = f64(unit) * cost
    return mxq(f64(w3), 0, "e4m3").T @ mxq(hid, 0, "e4m3")

@@ -1,0 +1,239 @@
+from contextlib import ExitStack
+
+import math
+
+import concourse.mybir as mybir
+from concourse.masks import make_identity
+
+K, T, S, N, H = 1024, 2048, 512, 128, 512
+FLOPS = 2 * (2 * K * H * S + H * N * S)
+
+F32 = mybir.dt.float32
+BF16 = mybir.dt.bfloat16
+I32 = mybir.dt.int32
+U32 = mybir.dt.uint32
+U16 = mybir.dt.uint16
+U8 = mybir.dt.uint8
+FP8X4 = mybir.dt.float8_e4m3fn_x4
+ALU = mybir.AluOpType
+ACT = mybir.ActivationFunctionType
+
+P = 128
+PACK = 4
+PASSES = K // (P * PACK)
+CLAMP = 20.0
+
+
+def tile_picked_ynewsv_cost_p_kernel(
+    tc, x_words, x_scales, w1, w2, pen, unit, w3, offs, nb1, nb2, out
+):
+    nc = tc.nc
+    with ExitStack() as ctx:
+        keep = ctx.enter_context(tc.tile_pool(name="keep", bufs=1))
+        work = ctx.enter_context(tc.tile_pool(name="work", bufs=2))
+        psum = ctx.enter_context(tc.psum_pool(name="psum", bufs=1))
+
+        def load_list(name, src):
+            lst = keep.tile([P, S // 16], U16, name=name)
+            nc.sync.dma_start(lst[:], src)
+            return lst
+
+        def load_weight(name, w, g, c0, width):
+            raw = keep.tile([P, PACK, width], F32, name=name)
+            rows = w[g * 512 : (g + 1) * 512, c0 : c0 + width]
+            nc.sync.dma_start(out=raw[:], in_=rows.rearrange("(p j) c -> p j c", j=PACK))
+            return raw
+
+        def load_words(g):
+            words = keep.tile([P, T], U32, name="x_words%d" % g)
+            nc.sync.dma_start(out=words[:].bitcast(I32), in_=x_words[g].rearrange("p n r -> p (n r)").bitcast(I32))
+            return words
+
+        def cast(copy, grouped, raw, c0, width):
+            dst = grouped[:].rearrange("p (t g q j) -> p g t q j", t=PACK, q=4, j=PACK)
+            copy(out=dst[:, c0 // 16 : (c0 + width) // 16], in_=raw[:].rearrange("p j (g t q) -> p g t q j", t=PACK, q=4))
+
+        def weight_tiles(name):
+            grouped = keep.tile([P, PACK * H], BF16, name=name + "_bf16", align_bytes=64)
+            codes = keep.tile([P, H], U32, name=name + "_codes", align_bytes=64)
+            scales = keep.tile([P, H], U8, name=name + "_scales", align_bytes=64)
+            return grouped, codes, scales
+
+        def quantize(tiles, c0, width):
+            grouped, codes, scales = tiles
+            nc.vector.quantize_mx(
+                out=codes[:, c0 : c0 + width].bitcast(FP8X4),
+                scales=scales[:, c0 : c0 + width],
+                in_=grouped[:, PACK * c0 : PACK * (c0 + width)],
+            )
+
+        half = H // 2
+
+        x_planes = keep.tile([P, T], U8, name="x_planes")
+        nc.vector.memset(x_planes[:].bitcast(I32), 0)
+        offs_t = load_list("offs_t", offs)
+        w1_raw0 = load_weight("w1_raw0", w1, 0, 0, H)
+        for q in range(4):
+            nc.sync.dma_start(
+                out=x_planes[32 * q : 32 * q + 4 * PASSES, :].bitcast(I32),
+                in_=x_scales[:, 4 * q : 4 * q + 4, :].bitcast(I32),
+            )
+        x_tab = [load_words(g) for g in range(PASSES)]
+        w1_raw1 = [load_weight("w1_raw1_%d" % h, w1, 1, h * half, half) for h in range(2)]
+        factors = keep.tile([P, 2, 16], F32, name="factors")
+        for n, vec in enumerate((pen, unit)):
+            runs = vec.rearrange("(g r) o -> g (r o)", r=16)
+            nc.sync.dma_start(out=factors[:, n, :], in_=runs.unsqueeze(1).to_broadcast([32, 4, 16]))
+        w2_raw0 = load_weight("w2_raw0", w2, 0, 0, H)
+        w2_raw1 = [load_weight("w2_raw1_%d" % h, w2, 1, h * half, half) for h in range(2)]
+        nb1_t = load_list("nb1_t", nb1)
+        nb2_t = load_list("nb2_t", nb2)
+        w3_raw = keep.tile([P, PACK, N], F32, name="w3_raw")
+        w3_rows = w3.rearrange("(g t q) m -> t g q m", t=PACK, q=4)
+        for t in range(PACK):
+            nc.sync.dma_start(out=w3_raw[:, t, :], in_=w3_rows[t])
+
+        identity = keep.tile([P, P], F32, name="identity")
+        make_identity(nc, identity[:])
+        own = keep.tile([P, 4], F32, name="own")
+        nc.vector.tensor_reduce(own[:], identity[:].rearrange("p (g q) -> p q g", q=4), mybir.AxisListType.X, ALU.add)
+        masked = keep.tile([P, 2 * PACK, 4], F32, name="masked")
+        nc.vector.tensor_tensor(
+            masked[:],
+            factors[:].rearrange("p n (t q) -> p (n t) q", q=4),
+            own[:].unsqueeze(1).to_broadcast([P, 2 * PACK, 4]),
+            ALU.mult,
+        )
+        picked = keep.tile([P, 2 * PACK], F32, name="picked")
+        nc.vector.tensor_reduce(picked[:], masked[:], mybir.AxisListType.X, ALU.add)
+        pen_t = picked[:, 0:PACK]
+        unit_t = picked[:, PACK : 2 * PACK]
+        sign = keep.tile([P, PACK], F32, name="sign")
+        step = keep.tile([P, PACK], F32, name="step")
+        size = keep.tile([P, PACK], F32, name="size")
+        gain = keep.tile([P, PACK], F32, name="gain")
+        neg_gain = keep.tile([P, PACK], F32, name="neg_gain")
+        neg_pen = keep.tile([P, PACK], F32, name="neg_pen")
+        slope = keep.tile([P, PACK], F32, name="slope")
+        share = keep.tile([P, PACK], F32, name="share")
+        nc.gpsimd.tensor_scalar(step[:], unit_t, 0.0, 2.0, ALU.is_ge, ALU.mult)
+        nc.gpsimd.tensor_scalar(sign[:], step[:], 1.0, -1.0, ALU.mult, ALU.add)
+        nc.gpsimd.tensor_tensor(size[:], unit_t, sign[:], ALU.mult)
+        nc.gpsimd.tensor_scalar(gain[:], size[:], 0.8, 0.0, ALU.mult, ALU.add)
+        nc.gpsimd.tensor_scalar(neg_gain[:], size[:], -0.8, 0.0, ALU.mult, ALU.add)
+        nc.gpsimd.tensor_scalar(neg_pen[:], pen_t, -1.0, 0.0, ALU.mult, ALU.add)
+        nc.gpsimd.tensor_tensor(slope[:], size[:], neg_pen[:], ALU.mult)
+        nc.gpsimd.tensor_scalar(share[:], pen_t, -1.25, 0.625, ALU.mult, ALU.add)
+
+        x_sc = keep.tile([P, S], U8, name="x_sc", align_bytes=64)
+        nc.vector.tensor_copy(x_sc[:], x_planes[:].indirect(offs_t[:]))
+        x_codes = [keep.tile([P, S], U32, name="x_codes%d" % g, align_bytes=64) for g in range(PASSES)]
+
+        def product(bank, tiles, g, t):
+            grouped, codes, scales = tiles
+            nc.tensor.matmul_mx(
+                out=bank[:],
+                lhsT=codes[:, t * P : (t + 1) * P].bitcast(FP8X4),
+                lhsT_scale=scales[:, t * P : (t + 1) * P],
+                rhs=x_codes[g][:].bitcast(FP8X4),
+                rhs_scale=x_sc[4 * g : P, :],
+                start=(g == 0),
+                stop=(g == PASSES - 1),
+            )
+
+        w1q = [weight_tiles("w1_%d" % g) for g in range(PASSES)]
+        w2q = [weight_tiles("w2_%d" % g) for g in range(PASSES)]
+        dm = [psum.tile([P, S], F32, name="dm%d" % t) for t in range(PACK)]
+        st = [psum.tile([P, S], F32, name="st%d" % t) for t in range(PACK)]
+
+        cast(nc.scalar.copy, w1q[0][0], w1_raw0, 0, H)
+        nc.vector.tensor_copy(x_codes[0][:], x_tab[0][:].indirect(offs_t[:]))
+        quantize(w1q[0], 0, H)
+        for t in range(PACK):
+            product(dm[t], w1q[0], 0, t)
+        nc.vector.tensor_copy(x_codes[1][:], x_tab[1][:].indirect(offs_t[:]))
+        cast(nc.scalar.copy, w1q[1][0], w1_raw1[0], 0, half)
+        cast(nc.vector.tensor_copy, w1q[1][0], w1_raw1[1], half, half)
+        for t in range(PACK):
+            quantize(w1q[1], t * P, P)
+            product(dm[t], w1q[1], 1, t)
+
+        grow = [keep.tile([P, S], F32, name="grow%d" % t) for t in range(PACK)]
+        over = [keep.tile([P, S], F32, name="over%d" % t) for t in range(PACK)]
+        for t in range(PACK):
+            nc.scalar.activation(grow[t][:], dm[t][:], ACT.Exp)
+        cast(nc.vector.tensor_copy, w2q[0][0], w2_raw0, 0, H)
+        quantize(w2q[0], 0, H)
+        for t in range(PACK):
+            product(st[t], w2q[0], 0, t)
+        for t in range(PACK):
+            nc.scalar.activation(over[t][:], dm[t][:], ACT.Relu, bias=-CLAMP)
+        cast(nc.vector.tensor_copy, w2q[1][0], w2_raw1[0], 0, half)
+        for t in range(PACK):
+            nc.vector.tensor_scalar(grow[t][:], grow[t][:], math.exp(CLAMP), 1.0, ALU.min, ALU.add)
+        cast(nc.vector.tensor_copy, w2q[1][0], w2_raw1[1], half, half)
+        for t in range(PACK):
+            quantize(w2q[1], t * P, P)
+            product(st[t], w2q[1], 1, t)
+
+        ratio = [keep.tile([P, S], F32, name="ratio%d" % t) for t in range(PACK)]
+        for t in range(PACK):
+            nc.scalar.activation(ratio[t][:], st[t][:], ACT.Sigmoid, scale=-1.0)
+        for t in range(PACK):
+            nc.vector.scalar_tensor_tensor(over[t][:], st[t][:], CLAMP, over[t][:], ALU.max, ALU.subtract)
+            nc.vector.scalar_tensor_tensor(ratio[t][:], ratio[t][:], 1.0 / (1.0 + math.exp(CLAMP)), grow[t][:], ALU.max, ALU.mult)
+
+        w3_bf16 = keep.tile([P, N, PACK], BF16, name="w3_bf16", align_bytes=64)
+        w3_codes = keep.tile([P, N], U32, name="w3_codes", align_bytes=64)
+        w3_scales = keep.tile([P, N], U8, name="w3_scales", align_bytes=64)
+        nc.vector.tensor_tensor(
+            w3_bf16[:], w3_raw[:].rearrange("p t m -> p m t"), sign[:].unsqueeze(1).to_broadcast([P, N, PACK]), ALU.mult
+        )
+        nc.vector.quantize_mx(
+            out=w3_codes[:].bitcast(FP8X4), scales=w3_scales[:], in_=w3_bf16[:].rearrange("p m t -> p (m t)")
+        )
+
+        hid = keep.tile([P, PACK, S], BF16, name="hid")
+        for t in range(PACK):
+            col = slice(t, t + 1)
+            window = keep.tile([P, 2 * S], F32, name="window%d" % t)
+            surplus = window[:, 0:S]
+            net = window[:, S : 2 * S]
+            log_ratio = work.tile([P, S], F32, name="log_ratio")
+            nc.scalar.activation(log_ratio[:], ratio[t][:], ACT.Ln)
+            nc.vector.scalar_tensor_tensor(net, over[t][:], CLAMP, log_ratio[:], ALU.subtract, ALU.subtract)
+            nc.scalar.activation(surplus, net, ACT.Relu, scale=gain[:, col])
+            second = work.tile([P, S], F32, name="second")
+            nc.scalar.activation(second[:], window[:].indirect(nb2_t[:]), ACT.Copy, scale=0.5)
+            base = work.tile([P, S], F32, name="base")
+            nc.vector.scalar_tensor_tensor(base[:], net, slope[:, col], surplus, ALU.mult, ALU.add)
+            offer = work.tile([P, S], F32, name="offer")
+            nc.vector.tensor_tensor(offer[:], window[:].indirect(nb1_t[:]), second[:], ALU.add)
+            moved = work.tile([P, S], F32, name="moved")
+            nc.vector.scalar_tensor_tensor(moved[:], net, neg_gain[:, col], offer[:], ALU.mult, ALU.min)
+            nc.vector.scalar_tensor_tensor(hid[:, t, :], moved[:], share[:, col], base[:], ALU.mult, ALU.add)
+
+        part = S // 2
+        for h in range(2):
+            cols = slice(h * part, (h + 1) * part)
+            woven = work.tile([P, part, PACK], BF16, name="woven", align_bytes=64)
+            copy = nc.vector.tensor_copy if h == 0 else nc.scalar.copy
+            copy(out=woven[:], in_=hid[:, :, cols].rearrange("p t j -> p j t"))
+            hid_codes = work.tile([P, part], U32, name="hid_codes", align_bytes=64)
+            hid_scales = work.tile([P, part], U8, name="hid_scales", align_bytes=64)
+            nc.vector.quantize_mx(
+                out=hid_codes[:].bitcast(FP8X4), scales=hid_scales[:], in_=woven[:].rearrange("p j t -> p (j t)")
+            )
+            acc = psum.tile([P, part], F32, name="dm%d" % h)
+            nc.tensor.matmul_mx(
+                out=acc[:],
+                lhsT=w3_codes[:].bitcast(FP8X4),
+                lhsT_scale=w3_scales[:],
+                rhs=hid_codes[:].bitcast(FP8X4),
+                rhs_scale=hid_scales[:],
+                start=True,
+                stop=True,
+            )
+            result = work.tile([P, part], F32, name="result")
+            nc.scalar.copy(out=result[:], in_=acc[:])
+            nc.sync.dma_start(out=out[:, cols], in_=result[:])

@@ -30,7 +30,7 @@ def tile_picked_ynewsv_cost_p_kernel(
     nc = tc.nc
     with ExitStack() as ctx:
         keep = ctx.enter_context(tc.tile_pool(name="keep", bufs=1))
-        work = ctx.enter_context(tc.tile_pool(name="work", bufs=2))
+        work = ctx.enter_context(tc.tile_pool(name="work", bufs=4))
         psum = ctx.enter_context(tc.psum_pool(name="psum", bufs=1))
 
         def load_list(name, src):
@@ -49,9 +49,10 @@ def tile_picked_ynewsv_cost_p_kernel(
             nc.sync.dma_start(out=words[:].bitcast(I32), in_=x_words[g].rearrange("p n r -> p (n r)").bitcast(I32))
             return words
 
-        def cast(copy, grouped, raw, c0, width):
+        def cast(copy, grouped, raw, c0, width, r0=0):
             dst = grouped[:].rearrange("p (t g q j) -> p g t q j", t=PACK, q=4, j=PACK)
-            copy(out=dst[:, c0 // 16 : (c0 + width) // 16], in_=raw[:].rearrange("p j (g t q) -> p g t q j", t=PACK, q=4))
+            src = raw[:].rearrange("p j (g t q) -> p g t q j", t=PACK, q=4)
+            copy(out=dst[:, c0 // 16 : (c0 + width) // 16], in_=src[:, r0 // 16 : (r0 + width) // 16])
 
         def weight_tiles(name):
             grouped = keep.tile([P, PACK * H], BF16, name=name + "_bf16", align_bytes=64)
@@ -79,13 +80,14 @@ def tile_picked_ynewsv_cost_p_kernel(
                 in_=x_scales[:, 4 * q : 4 * q + 4, :].bitcast(I32),
             )
         x_tab = [load_words(g) for g in range(PASSES)]
-        w1_raw1 = [load_weight("w1_raw1_%d" % h, w1, 1, h * half, half) for h in range(2)]
         factors = keep.tile([P, 2, 16], F32, name="factors")
         for n, vec in enumerate((pen, unit)):
             runs = vec.rearrange("(g r) o -> g (r o)", r=16)
-            nc.sync.dma_start(out=factors[:, n, :], in_=runs.unsqueeze(1).to_broadcast([32, 4, 16]))
-        w2_raw0 = load_weight("w2_raw0", w2, 0, 0, H)
-        w2_raw1 = [load_weight("w2_raw1_%d" % h, w2, 1, h * half, half) for h in range(2)]
+            nc.gpsimd.dma_start(out=factors[:, n, :], in_=runs.unsqueeze(1).to_broadcast([32, 4, 16]))
+        last_pieces = ((0, 256), (256, 128), (384, 128))
+        w1_raw1 = [load_weight("w1_raw1_%d" % c0, w1, 1, c0, width) for c0, width in last_pieces]
+        w2_raw0 = [load_weight("w2_raw0_%d" % h, w2, 0, h * half, half) for h in range(2)]
+        w2_raw1 = [load_weight("w2_raw1_%d" % c0, w2, 1, c0, width) for c0, width in last_pieces]
         nb1_t = load_list("nb1_t", nb1)
         nb2_t = load_list("nb2_t", nb2)
         w3_raw = keep.tile([P, PACK, N], F32, name="w3_raw")
@@ -98,14 +100,16 @@ def tile_picked_ynewsv_cost_p_kernel(
         own = keep.tile([P, 4], F32, name="own")
         nc.vector.tensor_reduce(own[:], identity[:].rearrange("p (g q) -> p q g", q=4), mybir.AxisListType.X, ALU.add)
         masked = keep.tile([P, 2 * PACK, 4], F32, name="masked")
-        nc.vector.tensor_tensor(
+        nc.gpsimd.tensor_tensor(
             masked[:],
             factors[:].rearrange("p n (t q) -> p (n t) q", q=4),
             own[:].unsqueeze(1).to_broadcast([P, 2 * PACK, 4]),
             ALU.mult,
         )
+        pairs = keep.tile([P, 2 * PACK, 2], F32, name="pairs")
+        nc.gpsimd.tensor_tensor(pairs[:], masked[:, :, 0:2], masked[:, :, 2:4], ALU.add)
         picked = keep.tile([P, 2 * PACK], F32, name="picked")
-        nc.vector.tensor_reduce(picked[:], masked[:], mybir.AxisListType.X, ALU.add)
+        nc.gpsimd.tensor_tensor(picked[:], pairs[:, :, 0], pairs[:, :, 1], ALU.add)
         pen_t = picked[:, 0:PACK]
         unit_t = picked[:, PACK : 2 * PACK]
         sign = keep.tile([P, PACK], F32, name="sign")
@@ -113,7 +117,7 @@ def tile_picked_ynewsv_cost_p_kernel(
         size = keep.tile([P, PACK], F32, name="size")
         gain = keep.tile([P, PACK], F32, name="gain")
         neg_gain = keep.tile([P, PACK], F32, name="neg_gain")
-        neg_pen = keep.tile([P, PACK], F32, name="neg_pen")
+        neg_size = keep.tile([P, PACK], F32, name="neg_size")
         slope = keep.tile([P, PACK], F32, name="slope")
         share = keep.tile([P, PACK], F32, name="share")
         nc.gpsimd.tensor_scalar(step[:], unit_t, 0.0, 2.0, ALU.is_ge, ALU.mult)
@@ -121,8 +125,8 @@ def tile_picked_ynewsv_cost_p_kernel(
         nc.gpsimd.tensor_tensor(size[:], unit_t, sign[:], ALU.mult)
         nc.gpsimd.tensor_scalar(gain[:], size[:], 0.8, 0.0, ALU.mult, ALU.add)
         nc.gpsimd.tensor_scalar(neg_gain[:], size[:], -0.8, 0.0, ALU.mult, ALU.add)
-        nc.gpsimd.tensor_scalar(neg_pen[:], pen_t, -1.0, 0.0, ALU.mult, ALU.add)
-        nc.gpsimd.tensor_tensor(slope[:], size[:], neg_pen[:], ALU.mult)
+        nc.gpsimd.tensor_scalar(neg_size[:], size[:], -1.0, 0.0, ALU.mult, ALU.add)
+        nc.gpsimd.tensor_tensor(slope[:], neg_size[:], pen_t, ALU.mult)
         nc.gpsimd.tensor_scalar(share[:], pen_t, -1.25, 0.625, ALU.mult, ALU.add)
 
         x_sc = keep.tile([P, S], U8, name="x_sc", align_bytes=64)
@@ -152,36 +156,34 @@ def tile_picked_ynewsv_cost_p_kernel(
         for t in range(PACK):
             product(dm[t], w1q[0], 0, t)
         nc.vector.tensor_copy(x_codes[1][:], x_tab[1][:].indirect(offs_t[:]))
-        cast(nc.scalar.copy, w1q[1][0], w1_raw1[0], 0, half)
-        cast(nc.vector.tensor_copy, w1q[1][0], w1_raw1[1], half, half)
+        for raw, (c0, width) in zip(w1_raw1, last_pieces):
+            cast(nc.scalar.copy if c0 == 0 else nc.vector.tensor_copy, w1q[1][0], raw, c0, width)
         for t in range(PACK):
             quantize(w1q[1], t * P, P)
             product(dm[t], w1q[1], 1, t)
 
         grow = [keep.tile([P, S], F32, name="grow%d" % t) for t in range(PACK)]
-        over = [keep.tile([P, S], F32, name="over%d" % t) for t in range(PACK)]
+        cast(nc.vector.tensor_copy, w2q[0][0], w2_raw0[0], 0, half)
         for t in range(PACK):
             nc.scalar.activation(grow[t][:], dm[t][:], ACT.Exp)
-        cast(nc.vector.tensor_copy, w2q[0][0], w2_raw0, 0, H)
+        cast(nc.vector.tensor_copy, w2q[0][0], w2_raw0[1], half, half)
         quantize(w2q[0], 0, H)
         for t in range(PACK):
             product(st[t], w2q[0], 0, t)
-        for t in range(PACK):
-            nc.scalar.activation(over[t][:], dm[t][:], ACT.Relu, bias=-CLAMP)
-        cast(nc.vector.tensor_copy, w2q[1][0], w2_raw1[0], 0, half)
-        for t in range(PACK):
-            nc.vector.tensor_scalar(grow[t][:], grow[t][:], math.exp(CLAMP), 1.0, ALU.min, ALU.add)
-        cast(nc.vector.tensor_copy, w2q[1][0], w2_raw1[1], half, half)
+        for raw, (c0, width) in zip(w2_raw1, last_pieces):
+            cast(nc.vector.tensor_copy, w2q[1][0], raw, c0, width)
         for t in range(PACK):
             quantize(w2q[1], t * P, P)
             product(st[t], w2q[1], 1, t)
 
+        one_plus = keep.tile([P, PACK * S], F32, name="w2_raw1_384")
+        for t in range(PACK):
+            nc.vector.tensor_scalar(one_plus[:, t * S : (t + 1) * S], grow[t][:], math.exp(CLAMP), 1.0, ALU.min, ALU.add)
         ratio = [keep.tile([P, S], F32, name="ratio%d" % t) for t in range(PACK)]
         for t in range(PACK):
             nc.scalar.activation(ratio[t][:], st[t][:], ACT.Sigmoid, scale=-1.0)
         for t in range(PACK):
-            nc.vector.scalar_tensor_tensor(over[t][:], st[t][:], CLAMP, over[t][:], ALU.max, ALU.subtract)
-            nc.vector.scalar_tensor_tensor(ratio[t][:], ratio[t][:], 1.0 / (1.0 + math.exp(CLAMP)), grow[t][:], ALU.max, ALU.mult)
+            nc.vector.scalar_tensor_tensor(ratio[t][:], ratio[t][:], 1.0 / (1.0 + math.exp(CLAMP)), one_plus[:, t * S : (t + 1) * S], ALU.max, ALU.mult)
 
         w3_bf16 = keep.tile([P, N, PACK], BF16, name="w3_bf16", align_bytes=64)
         w3_codes = keep.tile([P, N], U32, name="w3_codes", align_bytes=64)
@@ -194,30 +196,82 @@ def tile_picked_ynewsv_cost_p_kernel(
         )
 
         hid = keep.tile([P, PACK, S], BF16, name="hid")
-        for t in range(PACK):
-            col = slice(t, t + 1)
-            window = keep.tile([P, 2 * S], F32, name="window%d" % t)
-            surplus = window[:, 0:S]
-            net = window[:, S : 2 * S]
+        windows = [keep.tile([P, 2 * S], F32, name="window%d" % t) for t in range(PACK)]
+        lifted = [keep.tile([P, S], F32, name="lifted%d" % t) for t in range(PACK)]
+        first = [keep.tile([P, S], F32, name="first%d" % t) for t in range(PACK)]
+        second = [keep.tile([P, S], F32, name="second%d" % t) for t in range(PACK)]
+        base = [keep.tile([P, S], F32, name="base%d" % t) for t in range(PACK)]
+        offer = [keep.tile([P, S], F32, name="offer%d" % t) for t in range(PACK)]
+        moved = [keep.tile([P, S], F32, name="moved%d" % t) for t in range(PACK)]
+
+        def lift(t):
             log_ratio = work.tile([P, S], F32, name="log_ratio")
             nc.scalar.activation(log_ratio[:], ratio[t][:], ACT.Ln)
-            nc.vector.scalar_tensor_tensor(net, over[t][:], CLAMP, log_ratio[:], ALU.subtract, ALU.subtract)
-            nc.scalar.activation(surplus, net, ACT.Relu, scale=gain[:, col])
-            second = work.tile([P, S], F32, name="second")
-            nc.scalar.activation(second[:], window[:].indirect(nb2_t[:]), ACT.Copy, scale=0.5)
-            base = work.tile([P, S], F32, name="base")
-            nc.vector.scalar_tensor_tensor(base[:], net, slope[:, col], surplus, ALU.mult, ALU.add)
-            offer = work.tile([P, S], F32, name="offer")
-            nc.vector.tensor_tensor(offer[:], window[:].indirect(nb1_t[:]), second[:], ALU.add)
-            moved = work.tile([P, S], F32, name="moved")
-            nc.vector.scalar_tensor_tensor(moved[:], net, neg_gain[:, col], offer[:], ALU.mult, ALU.min)
-            nc.vector.scalar_tensor_tensor(hid[:, t, :], moved[:], share[:, col], base[:], ALU.mult, ALU.add)
+            nc.vector.scalar_tensor_tensor(lifted[t][:], dm[t][:], CLAMP, log_ratio[:], ALU.max, ALU.add)
+
+        def net_stock(t):
+            nc.vector.scalar_tensor_tensor(windows[t][:, S:], st[t][:], CLAMP, lifted[t][:], ALU.max, ALU.subtract)
+
+        def surplus_of(t):
+            nc.scalar.activation(windows[t][:, :S], windows[t][:, S:], ACT.Relu, scale=gain[:, t : t + 1])
+
+        def fetch(t, c0, c1):
+            entries = slice(c0 // 16, c1 // 16)
+            nc.scalar.activation(second[t][:, c0:c1], windows[t][:].indirect(nb2_t[:, entries]), ACT.Copy, scale=0.5)
+            if t > 0:
+                nc.scalar.activation(first[t][:, c0:c1], windows[t][:].indirect(nb1_t[:, entries]), ACT.Copy)
+
+        def base_of(t):
+            nc.vector.scalar_tensor_tensor(
+                base[t][:], windows[t][:, S:], slope[:, t : t + 1], windows[t][:, :S], ALU.mult, ALU.add
+            )
+
+        def offer_of(t, c0, c1):
+            source = first[t][:, c0:c1] if t > 0 else windows[t][:].indirect(nb1_t[:, c0 // 16 : c1 // 16])
+            nc.vector.tensor_tensor(offer[t][:, c0:c1], source, second[t][:, c0:c1], ALU.add)
+
+        def moved_of(t, c0, c1):
+            nc.vector.scalar_tensor_tensor(
+                moved[t][:, c0:c1], windows[t][:, S + c0 : S + c1], neg_gain[:, t : t + 1], offer[t][:, c0:c1], ALU.mult, ALU.min
+            )
+
+        def hid_of(t, c0, c1):
+            nc.vector.scalar_tensor_tensor(
+                hid[:, t, c0:c1], moved[t][:, c0:c1], share[:, t : t + 1], base[t][:, c0:c1], ALU.mult, ALU.add
+            )
+
+        last = PACK - 1
+        lift(0)
+        for t in range(PACK):
+            if t < last:
+                lift(t + 1)
+            net_stock(t)
+        surplus_of(0)
+        base_of(0)
+        for t in range(last):
+            fetch(t, 0, S)
+            surplus_of(t + 1)
+            offer_of(t, 0, S)
+            if t > 0:
+                hid_of(t - 1, 0, S)
+            base_of(t + 1)
+            moved_of(t, 0, S)
+        halves = ((0, S // 2), (S // 2, S))
+        for c0, c1 in halves:
+            fetch(last, c0, c1)
+        offer_of(last, *halves[0])
+        hid_of(last - 1, 0, S)
+        moved_of(last, *halves[0])
+        offer_of(last, *halves[1])
+        hid_of(last, *halves[0])
+        moved_of(last, *halves[1])
+        hid_of(last, *halves[1])
 
         part = S // 2
         for h in range(2):
             cols = slice(h * part, (h + 1) * part)
             woven = work.tile([P, part, PACK], BF16, name="woven", align_bytes=64)
-            copy = nc.vector.tensor_copy if h == 0 else nc.scalar.copy
+            copy = nc.scalar.copy if h == 0 else nc.vector.tensor_copy
             copy(out=woven[:], in_=hid[:, :, cols].rearrange("p t j -> p j t"))
             hid_codes = work.tile([P, part], U32, name="hid_codes", align_bytes=64)
             hid_scales = work.tile([P, part], U8, name="hid_scales", align_bytes=64)

@@ -84,9 +84,9 @@ def tile_picked_ynewsv_cost_p_kernel(
         for n, vec in enumerate((pen, unit)):
             runs = vec.rearrange("(g r) o -> g (r o)", r=16)
             nc.gpsimd.dma_start(out=factors[:, n, :], in_=runs.unsqueeze(1).to_broadcast([32, 4, 16]))
-        last_pieces = ((0, 256), (256, 128), (384, 128))
-        w1_raw1 = [load_weight("w1_raw1_%d" % c0, w1, 1, c0, width) for c0, width in last_pieces]
-        w2_raw0 = [load_weight("w2_raw0_%d" % h, w2, 0, h * half, half) for h in range(2)]
+        last_pieces = ((0, half), (half, half))
+        w1_raw1 = load_weight("w1_raw1", w1, 1, 0, H)
+        w2_raw0 = load_weight("w2_raw0", w2, 0, 0, H)
         w2_raw1 = [load_weight("w2_raw1_%d" % c0, w2, 1, c0, width) for c0, width in last_pieces]
         nb1_t = load_list("nb1_t", nb1)
         nb2_t = load_list("nb2_t", nb2)
@@ -112,7 +112,7 @@ def tile_picked_ynewsv_cost_p_kernel(
         nc.gpsimd.tensor_tensor(picked[:], pairs[:, :, 0], pairs[:, :, 1], ALU.add)
         pen_t = picked[:, 0:PACK]
         unit_t = picked[:, PACK : 2 * PACK]
-        sign = keep.tile([P, PACK], F32, name="sign")
+        sign = keep.tile([P, PACK], BF16, name="sign")
         step = keep.tile([P, PACK], F32, name="step")
         size = keep.tile([P, PACK], F32, name="size")
         gain = keep.tile([P, PACK], F32, name="gain")
@@ -156,17 +156,16 @@ def tile_picked_ynewsv_cost_p_kernel(
         for t in range(PACK):
             product(dm[t], w1q[0], 0, t)
         nc.vector.tensor_copy(x_codes[1][:], x_tab[1][:].indirect(offs_t[:]))
-        for raw, (c0, width) in zip(w1_raw1, last_pieces):
-            cast(nc.scalar.copy if c0 == 0 else nc.vector.tensor_copy, w1q[1][0], raw, c0, width)
+        cast(nc.vector.tensor_copy, w1q[1][0], w1_raw1, 0, 352)
+        cast(nc.scalar.copy, w1q[1][0], w1_raw1, 352, H - 352, 352)
         for t in range(PACK):
             quantize(w1q[1], t * P, P)
             product(dm[t], w1q[1], 1, t)
 
         grow = [keep.tile([P, S], F32, name="grow%d" % t) for t in range(PACK)]
-        cast(nc.vector.tensor_copy, w2q[0][0], w2_raw0[0], 0, half)
         for t in range(PACK):
             nc.scalar.activation(grow[t][:], dm[t][:], ACT.Exp)
-        cast(nc.vector.tensor_copy, w2q[0][0], w2_raw0[1], half, half)
+        cast(nc.vector.tensor_copy, w2q[0][0], w2_raw0, 0, H)
         quantize(w2q[0], 0, H)
         for t in range(PACK):
             product(st[t], w2q[0], 0, t)
@@ -176,7 +175,7 @@ def tile_picked_ynewsv_cost_p_kernel(
             quantize(w2q[1], t * P, P)
             product(st[t], w2q[1], 1, t)
 
-        one_plus = keep.tile([P, PACK * S], F32, name="w2_raw1_384")
+        one_plus = keep.tile([P, PACK * S], F32, name="w2_raw1_256")
         for t in range(PACK):
             nc.vector.tensor_scalar(one_plus[:, t * S : (t + 1) * S], grow[t][:], math.exp(CLAMP), 1.0, ALU.min, ALU.add)
         ratio = [keep.tile([P, S], F32, name="ratio%d" % t) for t in range(PACK)]
@@ -188,9 +187,9 @@ def tile_picked_ynewsv_cost_p_kernel(
         w3_bf16 = keep.tile([P, N, PACK], BF16, name="w3_bf16", align_bytes=64)
         w3_codes = keep.tile([P, N], U32, name="w3_codes", align_bytes=64)
         w3_scales = keep.tile([P, N], U8, name="w3_scales", align_bytes=64)
-        nc.vector.tensor_tensor(
-            w3_bf16[:], w3_raw[:].rearrange("p t m -> p m t"), sign[:].unsqueeze(1).to_broadcast([P, N, PACK]), ALU.mult
-        )
+        w3_woven = keep.tile([P, N, PACK], BF16, name="w3_woven")
+        nc.vector.tensor_copy(w3_woven[:], w3_raw[:].rearrange("p t m -> p m t"))
+        nc.vector.tensor_tensor(w3_bf16[:], w3_woven[:], sign[:].unsqueeze(1).to_broadcast([P, N, PACK]), ALU.mult)
         nc.vector.quantize_mx(
             out=w3_codes[:].bitcast(FP8X4), scales=w3_scales[:], in_=w3_bf16[:].rearrange("p m t -> p (m t)")
         )

@@ -71,11 +71,11 @@ def tile_picked_ynewsv_cost_p_kernel(
         half = H // 2
 
         x_planes = keep.tile([P, T], U8, name="x_planes")
-        nc.vector.memset(x_planes[:].bitcast(I32), 0)
+        nc.gpsimd.memset(x_planes[:].bitcast(I32), 0)
         offs_t = load_list("offs_t", offs)
         w1_raw0 = load_weight("w1_raw0", w1, 0, 0, H)
         for q in range(4):
-            nc.sync.dma_start(
+            nc.gpsimd.dma_start(
                 out=x_planes[32 * q : 32 * q + 4 * PASSES, :].bitcast(I32),
                 in_=x_scales[:, 4 * q : 4 * q + 4, :].bitcast(I32),
             )
@@ -259,11 +259,12 @@ def tile_picked_ynewsv_cost_p_kernel(
         for c0, c1 in halves:
             fetch(last, c0, c1)
         offer_of(last, *halves[0])
-        hid_of(last - 1, 0, S)
+        hid_of(last - 1, *halves[0])
         moved_of(last, *halves[0])
         offer_of(last, *halves[1])
         hid_of(last, *halves[0])
         moved_of(last, *halves[1])
+        hid_of(last - 1, *halves[1])
         hid_of(last, *halves[1])
 
         part = S // 2
@@ -288,5 +289,6 @@ def tile_picked_ynewsv_cost_p_kernel(
                 stop=True,
             )
             result = work.tile([P, part], F32, name="result")
-            nc.scalar.copy(out=result[:], in_=acc[:])
+            evict = nc.scalar.copy if h == 0 else nc.vector.tensor_copy
+            evict(out=result[:], in_=acc[:])
             nc.sync.dma_start(out=out[:, cols], in_=result[:])

@@ -1,6 +1,5 @@
-from contextlib import ExitStack
-
 import math
+from contextlib import ExitStack
 
 import concourse.mybir as mybir
 from concourse.masks import make_identity
@@ -20,8 +19,14 @@ ACT = mybir.ActivationFunctionType
 
 P = 128
 PACK = 4
-PASSES = K // (P * PACK)
+K_PASS = P * PACK
+PASSES = K // K_PASS
+RUN = 4
+GROUP = PACK * RUN
+PER_COLUMN = 16
 CLAMP = 20.0
+W1_VECTOR_COLUMNS = 352
+WORK_BUFS = 4
 
 
 def tile_picked_ynewsv_cost_p_kernel(
@@ -30,17 +35,17 @@ def tile_picked_ynewsv_cost_p_kernel(
     nc = tc.nc
     with ExitStack() as ctx:
         keep = ctx.enter_context(tc.tile_pool(name="keep", bufs=1))
-        work = ctx.enter_context(tc.tile_pool(name="work", bufs=4))
+        work = ctx.enter_context(tc.tile_pool(name="work", bufs=WORK_BUFS))
         psum = ctx.enter_context(tc.psum_pool(name="psum", bufs=1))
 
         def load_list(name, src):
-            lst = keep.tile([P, S // 16], U16, name=name)
-            nc.sync.dma_start(lst[:], src)
-            return lst
+            entries = keep.tile([P, S // PER_COLUMN], U16, name=name)
+            nc.sync.dma_start(entries[:], src)
+            return entries
 
         def load_weight(name, w, g, c0, width):
             raw = keep.tile([P, PACK, width], F32, name=name)
-            rows = w[g * 512 : (g + 1) * 512, c0 : c0 + width]
+            rows = w[g * K_PASS : (g + 1) * K_PASS, c0 : c0 + width]
             nc.sync.dma_start(out=raw[:], in_=rows.rearrange("(p j) c -> p j c", j=PACK))
             return raw
 
@@ -50,9 +55,9 @@ def tile_picked_ynewsv_cost_p_kernel(
             return words
 
         def cast(copy, grouped, raw, c0, width, r0=0):
-            dst = grouped[:].rearrange("p (t g q j) -> p g t q j", t=PACK, q=4, j=PACK)
-            src = raw[:].rearrange("p j (g t q) -> p g t q j", t=PACK, q=4)
-            copy(out=dst[:, c0 // 16 : (c0 + width) // 16], in_=src[:, r0 // 16 : (r0 + width) // 16])
+            dst = grouped[:].rearrange("p (t u q j) -> p u t q j", t=PACK, q=RUN, j=PACK)
+            src = raw[:].rearrange("p j (u t q) -> p u t q j", t=PACK, q=RUN)
+            copy(out=dst[:, c0 // GROUP : (c0 + width) // GROUP], in_=src[:, r0 // GROUP : (r0 + width) // GROUP])
 
         def weight_tiles(name):
             grouped = keep.tile([P, PACK * H], BF16, name=name + "_bf16", align_bytes=64)
@@ -60,58 +65,57 @@ def tile_picked_ynewsv_cost_p_kernel(
             scales = keep.tile([P, H], U8, name=name + "_scales", align_bytes=64)
             return grouped, codes, scales
 
-        def quantize(tiles, c0, width):
+        def quantize(tiles, word0, words):
             grouped, codes, scales = tiles
             nc.vector.quantize_mx(
-                out=codes[:, c0 : c0 + width].bitcast(FP8X4),
-                scales=scales[:, c0 : c0 + width],
-                in_=grouped[:, PACK * c0 : PACK * (c0 + width)],
+                out=codes[:, word0 : word0 + words].bitcast(FP8X4),
+                scales=scales[:, word0 : word0 + words],
+                in_=grouped[:, PACK * word0 : PACK * (word0 + words)],
             )
 
-        half = H // 2
-
-        x_planes = keep.tile([P, T], U8, name="x_planes")
-        nc.gpsimd.memset(x_planes[:].bitcast(I32), 0)
-        offs_t = load_list("offs_t", offs)
+        x_scale_table = keep.tile([P, T], U8, name="x_scale_table")
+        nc.vector.memset(x_scale_table[:].bitcast(I32), 0)
+        offs_list = load_list("offs_list", offs)
         w1_raw0 = load_weight("w1_raw0", w1, 0, 0, H)
-        for q in range(4):
-            nc.gpsimd.dma_start(
-                out=x_planes[32 * q : 32 * q + 4 * PASSES, :].bitcast(I32),
-                in_=x_scales[:, 4 * q : 4 * q + 4, :].bitcast(I32),
+        for quadrant in range(4):
+            nc.sync.dma_start(
+                out=x_scale_table[32 * quadrant : 32 * quadrant + 4 * PASSES, :].bitcast(I32),
+                in_=x_scales[:, 4 * quadrant : 4 * quadrant + 4, :].bitcast(I32),
             )
-        x_tab = [load_words(g) for g in range(PASSES)]
-        factors = keep.tile([P, 2, 16], F32, name="factors")
+        x_word_tables = [load_words(g) for g in range(PASSES)]
+        factors = keep.tile([P, 2, GROUP], F32, name="factors")
         for n, vec in enumerate((pen, unit)):
-            runs = vec.rearrange("(g r) o -> g (r o)", r=16)
-            nc.gpsimd.dma_start(out=factors[:, n, :], in_=runs.unsqueeze(1).to_broadcast([32, 4, 16]))
-        last_pieces = ((0, half), (half, half))
+            groups = vec.rearrange("(u r) o -> u (r o)", r=GROUP)
+            nc.gpsimd.dma_start(out=factors[:, n, :], in_=groups.unsqueeze(1).to_broadcast([P // RUN, RUN, GROUP]))
         w1_raw1 = load_weight("w1_raw1", w1, 1, 0, H)
         w2_raw0 = load_weight("w2_raw0", w2, 0, 0, H)
-        w2_raw1 = [load_weight("w2_raw1_%d" % c0, w2, 1, c0, width) for c0, width in last_pieces]
-        nb1_t = load_list("nb1_t", nb1)
-        nb2_t = load_list("nb2_t", nb2)
+        last_pieces = ((0, H // 2), (H // 2, H // 2))
+        last_piece_names = ["w2_raw1_%d" % c0 for c0, width in last_pieces]
+        w2_raw1 = [load_weight(name, w2, 1, c0, width) for name, (c0, width) in zip(last_piece_names, last_pieces)]
+        nb1_list = load_list("nb1_list", nb1)
+        nb2_list = load_list("nb2_list", nb2)
         w3_raw = keep.tile([P, PACK, N], F32, name="w3_raw")
-        w3_rows = w3.rearrange("(g t q) m -> t g q m", t=PACK, q=4)
+        w3_rows = w3.rearrange("(u t q) m -> t u q m", t=PACK, q=RUN)
         for t in range(PACK):
             nc.sync.dma_start(out=w3_raw[:, t, :], in_=w3_rows[t])
 
         identity = keep.tile([P, P], F32, name="identity")
         make_identity(nc, identity[:])
-        own = keep.tile([P, 4], F32, name="own")
-        nc.vector.tensor_reduce(own[:], identity[:].rearrange("p (g q) -> p q g", q=4), mybir.AxisListType.X, ALU.add)
-        masked = keep.tile([P, 2 * PACK, 4], F32, name="masked")
+        own = keep.tile([P, RUN], F32, name="own")
+        nc.vector.tensor_reduce(own[:], identity[:].rearrange("p (u q) -> p q u", q=RUN), mybir.AxisListType.X, ALU.add)
+        masked = keep.tile([P, 2 * PACK, RUN], F32, name="masked")
         nc.gpsimd.tensor_tensor(
             masked[:],
-            factors[:].rearrange("p n (t q) -> p (n t) q", q=4),
-            own[:].unsqueeze(1).to_broadcast([P, 2 * PACK, 4]),
+            factors[:].rearrange("p n (t q) -> p (n t) q", q=RUN),
+            own[:].unsqueeze(1).to_broadcast([P, 2 * PACK, RUN]),
             ALU.mult,
         )
         pairs = keep.tile([P, 2 * PACK, 2], F32, name="pairs")
         nc.gpsimd.tensor_tensor(pairs[:], masked[:, :, 0:2], masked[:, :, 2:4], ALU.add)
         picked = keep.tile([P, 2 * PACK], F32, name="picked")
         nc.gpsimd.tensor_tensor(picked[:], pairs[:, :, 0], pairs[:, :, 1], ALU.add)
-        pen_t = picked[:, 0:PACK]
-        unit_t = picked[:, PACK : 2 * PACK]
+        pen_own = picked[:, 0:PACK]
+        unit_own = picked[:, PACK : 2 * PACK]
         sign = keep.tile([P, PACK], BF16, name="sign")
         step = keep.tile([P, PACK], F32, name="step")
         size = keep.tile([P, PACK], F32, name="size")
@@ -120,17 +124,17 @@ def tile_picked_ynewsv_cost_p_kernel(
         neg_size = keep.tile([P, PACK], F32, name="neg_size")
         slope = keep.tile([P, PACK], F32, name="slope")
         share = keep.tile([P, PACK], F32, name="share")
-        nc.gpsimd.tensor_scalar(step[:], unit_t, 0.0, 2.0, ALU.is_ge, ALU.mult)
+        nc.gpsimd.tensor_scalar(step[:], unit_own, 0.0, 2.0, ALU.is_ge, ALU.mult)
         nc.gpsimd.tensor_scalar(sign[:], step[:], 1.0, -1.0, ALU.mult, ALU.add)
-        nc.gpsimd.tensor_tensor(size[:], unit_t, sign[:], ALU.mult)
+        nc.gpsimd.tensor_tensor(size[:], unit_own, sign[:], ALU.mult)
         nc.gpsimd.tensor_scalar(gain[:], size[:], 0.8, 0.0, ALU.mult, ALU.add)
         nc.gpsimd.tensor_scalar(neg_gain[:], size[:], -0.8, 0.0, ALU.mult, ALU.add)
         nc.gpsimd.tensor_scalar(neg_size[:], size[:], -1.0, 0.0, ALU.mult, ALU.add)
-        nc.gpsimd.tensor_tensor(slope[:], neg_size[:], pen_t, ALU.mult)
-        nc.gpsimd.tensor_scalar(share[:], pen_t, -1.25, 0.625, ALU.mult, ALU.add)
+        nc.gpsimd.tensor_tensor(slope[:], neg_size[:], pen_own, ALU.mult)
+        nc.gpsimd.tensor_scalar(share[:], pen_own, -1.25, 0.625, ALU.mult, ALU.add)
 
-        x_sc = keep.tile([P, S], U8, name="x_sc", align_bytes=64)
-        nc.vector.tensor_copy(x_sc[:], x_planes[:].indirect(offs_t[:]))
+        x_scale_rows = keep.tile([P, S], U8, name="x_scale_rows", align_bytes=64)
+        nc.vector.tensor_copy(x_scale_rows[:], x_scale_table[:].indirect(offs_list[:]))
         x_codes = [keep.tile([P, S], U32, name="x_codes%d" % g, align_bytes=64) for g in range(PASSES)]
 
         def product(bank, tiles, g, t):
@@ -140,49 +144,52 @@ def tile_picked_ynewsv_cost_p_kernel(
                 lhsT=codes[:, t * P : (t + 1) * P].bitcast(FP8X4),
                 lhsT_scale=scales[:, t * P : (t + 1) * P],
                 rhs=x_codes[g][:].bitcast(FP8X4),
-                rhs_scale=x_sc[4 * g : P, :],
+                rhs_scale=x_scale_rows[4 * g : P, :],
                 start=(g == 0),
                 stop=(g == PASSES - 1),
             )
 
-        w1q = [weight_tiles("w1_%d" % g) for g in range(PASSES)]
-        w2q = [weight_tiles("w2_%d" % g) for g in range(PASSES)]
-        dm = [psum.tile([P, S], F32, name="dm%d" % t) for t in range(PACK)]
+        w1_mx = [weight_tiles("w1_%d" % g) for g in range(PASSES)]
+        w2_mx = [weight_tiles("w2_%d" % g) for g in range(PASSES)]
+        dm_names = ["dm%d" % t for t in range(PACK)]
+        dm = [psum.tile([P, S], F32, name=name) for name in dm_names]
         st = [psum.tile([P, S], F32, name="st%d" % t) for t in range(PACK)]
 
-        cast(nc.scalar.copy, w1q[0][0], w1_raw0, 0, H)
-        nc.vector.tensor_copy(x_codes[0][:], x_tab[0][:].indirect(offs_t[:]))
-        quantize(w1q[0], 0, H)
+        cast(nc.scalar.copy, w1_mx[0][0], w1_raw0, 0, H)
+        nc.vector.tensor_copy(x_codes[0][:], x_word_tables[0][:].indirect(offs_list[:]))
+        quantize(w1_mx[0], 0, H)
         for t in range(PACK):
-            product(dm[t], w1q[0], 0, t)
-        nc.vector.tensor_copy(x_codes[1][:], x_tab[1][:].indirect(offs_t[:]))
-        cast(nc.vector.tensor_copy, w1q[1][0], w1_raw1, 0, 352)
-        cast(nc.scalar.copy, w1q[1][0], w1_raw1, 352, H - 352, 352)
+            product(dm[t], w1_mx[0], 0, t)
+        nc.vector.tensor_copy(x_codes[1][:], x_word_tables[1][:].indirect(offs_list[:]))
+        cast(nc.vector.tensor_copy, w1_mx[1][0], w1_raw1, 0, W1_VECTOR_COLUMNS)
+        cast(nc.scalar.copy, w1_mx[1][0], w1_raw1, W1_VECTOR_COLUMNS, H - W1_VECTOR_COLUMNS, W1_VECTOR_COLUMNS)
         for t in range(PACK):
-            quantize(w1q[1], t * P, P)
-            product(dm[t], w1q[1], 1, t)
+            quantize(w1_mx[1], t * P, P)
+            product(dm[t], w1_mx[1], 1, t)
 
-        grow = [keep.tile([P, S], F32, name="grow%d" % t) for t in range(PACK)]
+        exp_dm = [keep.tile([P, S], F32, name="exp_dm%d" % t) for t in range(PACK)]
         for t in range(PACK):
-            nc.scalar.activation(grow[t][:], dm[t][:], ACT.Exp)
-        cast(nc.vector.tensor_copy, w2q[0][0], w2_raw0, 0, H)
-        quantize(w2q[0], 0, H)
+            nc.scalar.activation(exp_dm[t][:], dm[t][:], ACT.Exp)
+        cast(nc.vector.tensor_copy, w2_mx[0][0], w2_raw0, 0, H)
+        quantize(w2_mx[0], 0, H)
         for t in range(PACK):
-            product(st[t], w2q[0], 0, t)
+            product(st[t], w2_mx[0], 0, t)
         for raw, (c0, width) in zip(w2_raw1, last_pieces):
-            cast(nc.vector.tensor_copy, w2q[1][0], raw, c0, width)
+            cast(nc.vector.tensor_copy, w2_mx[1][0], raw, c0, width)
         for t in range(PACK):
-            quantize(w2q[1], t * P, P)
-            product(st[t], w2q[1], 1, t)
+            quantize(w2_mx[1], t * P, P)
+            product(st[t], w2_mx[1], 1, t)
 
-        one_plus = keep.tile([P, PACK * S], F32, name="w2_raw1_256")
+        one_plus = keep.tile([P, PACK * S], F32, name=last_piece_names[-1])
         for t in range(PACK):
-            nc.vector.tensor_scalar(one_plus[:, t * S : (t + 1) * S], grow[t][:], math.exp(CLAMP), 1.0, ALU.min, ALU.add)
+            nc.vector.tensor_scalar(one_plus[:, t * S : (t + 1) * S], exp_dm[t][:], math.exp(CLAMP), 1.0, ALU.min, ALU.add)
         ratio = [keep.tile([P, S], F32, name="ratio%d" % t) for t in range(PACK)]
         for t in range(PACK):
             nc.scalar.activation(ratio[t][:], st[t][:], ACT.Sigmoid, scale=-1.0)
         for t in range(PACK):
-            nc.vector.scalar_tensor_tensor(ratio[t][:], ratio[t][:], 1.0 / (1.0 + math.exp(CLAMP)), one_plus[:, t * S : (t + 1) * S], ALU.max, ALU.mult)
+            nc.vector.scalar_tensor_tensor(
+                ratio[t][:], ratio[t][:], 1.0 / (1.0 + math.exp(CLAMP)), one_plus[:, t * S : (t + 1) * S], ALU.max, ALU.mult
+            )
 
         w3_bf16 = keep.tile([P, N, PACK], BF16, name="w3_bf16", align_bytes=64)
         w3_codes = keep.tile([P, N], U32, name="w3_codes", align_bytes=64)
@@ -197,7 +204,7 @@ def tile_picked_ynewsv_cost_p_kernel(
         hid = keep.tile([P, PACK, S], BF16, name="hid")
         windows = [keep.tile([P, 2 * S], F32, name="window%d" % t) for t in range(PACK)]
         lifted = [keep.tile([P, S], F32, name="lifted%d" % t) for t in range(PACK)]
-        first = [keep.tile([P, S], F32, name="first%d" % t) for t in range(PACK)]
+        first = {t: keep.tile([P, S], F32, name="first%d" % t) for t in range(1, PACK, 2)}
         second = [keep.tile([P, S], F32, name="second%d" % t) for t in range(PACK)]
         base = [keep.tile([P, S], F32, name="base%d" % t) for t in range(PACK)]
         offer = [keep.tile([P, S], F32, name="offer%d" % t) for t in range(PACK)]
@@ -208,17 +215,17 @@ def tile_picked_ynewsv_cost_p_kernel(
             nc.scalar.activation(log_ratio[:], ratio[t][:], ACT.Ln)
             nc.vector.scalar_tensor_tensor(lifted[t][:], dm[t][:], CLAMP, log_ratio[:], ALU.max, ALU.add)
 
-        def net_stock(t):
+        def net_of(t):
             nc.vector.scalar_tensor_tensor(windows[t][:, S:], st[t][:], CLAMP, lifted[t][:], ALU.max, ALU.subtract)
 
         def surplus_of(t):
             nc.scalar.activation(windows[t][:, :S], windows[t][:, S:], ACT.Relu, scale=gain[:, t : t + 1])
 
         def fetch(t, c0, c1):
-            entries = slice(c0 // 16, c1 // 16)
-            nc.scalar.activation(second[t][:, c0:c1], windows[t][:].indirect(nb2_t[:, entries]), ACT.Copy, scale=0.5)
-            if t > 0:
-                nc.scalar.activation(first[t][:, c0:c1], windows[t][:].indirect(nb1_t[:, entries]), ACT.Copy)
+            entries = slice(c0 // PER_COLUMN, c1 // PER_COLUMN)
+            nc.scalar.activation(second[t][:, c0:c1], windows[t][:].indirect(nb2_list[:, entries]), ACT.Copy, scale=0.5)
+            if t in first:
+                nc.scalar.activation(first[t][:, c0:c1], windows[t][:].indirect(nb1_list[:, entries]), ACT.Copy)
 
         def base_of(t):
             nc.vector.scalar_tensor_tensor(
@@ -226,12 +233,14 @@ def tile_picked_ynewsv_cost_p_kernel(
             )
 
         def offer_of(t, c0, c1):
-            source = first[t][:, c0:c1] if t > 0 else windows[t][:].indirect(nb1_t[:, c0 // 16 : c1 // 16])
+            entries = slice(c0 // PER_COLUMN, c1 // PER_COLUMN)
+            source = first[t][:, c0:c1] if t in first else windows[t][:].indirect(nb1_list[:, entries])
             nc.vector.tensor_tensor(offer[t][:, c0:c1], source, second[t][:, c0:c1], ALU.add)
 
         def moved_of(t, c0, c1):
+            net = windows[t][:, S + c0 : S + c1]
             nc.vector.scalar_tensor_tensor(
-                moved[t][:, c0:c1], windows[t][:, S + c0 : S + c1], neg_gain[:, t : t + 1], offer[t][:, c0:c1], ALU.mult, ALU.min
+                moved[t][:, c0:c1], net, neg_gain[:, t : t + 1], offer[t][:, c0:c1], ALU.mult, ALU.min
             )
 
         def hid_of(t, c0, c1):
@@ -244,7 +253,7 @@ def tile_picked_ynewsv_cost_p_kernel(
         for t in range(PACK):
             if t < last:
                 lift(t + 1)
-            net_stock(t)
+            net_of(t)
         surplus_of(0)
         base_of(0)
         for t in range(last):
@@ -267,18 +276,16 @@ def tile_picked_ynewsv_cost_p_kernel(
         hid_of(last - 1, *halves[1])
         hid_of(last, *halves[1])
 
-        part = S // 2
-        for h in range(2):
-            cols = slice(h * part, (h + 1) * part)
-            woven = work.tile([P, part, PACK], BF16, name="woven", align_bytes=64)
-            copy = nc.scalar.copy if h == 0 else nc.vector.tensor_copy
-            copy(out=woven[:], in_=hid[:, :, cols].rearrange("p t j -> p j t"))
-            hid_codes = work.tile([P, part], U32, name="hid_codes", align_bytes=64)
-            hid_scales = work.tile([P, part], U8, name="hid_scales", align_bytes=64)
+        for (c0, c1), copy, bank_name in zip(halves, (nc.scalar.copy, nc.vector.tensor_copy), dm_names):
+            width = c1 - c0
+            woven = work.tile([P, width, PACK], BF16, name="woven", align_bytes=64)
+            copy(out=woven[:], in_=hid[:, :, c0:c1].rearrange("p t j -> p j t"))
+            hid_codes = work.tile([P, width], U32, name="hid_codes", align_bytes=64)
+            hid_scales = work.tile([P, width], U8, name="hid_scales", align_bytes=64)
             nc.vector.quantize_mx(
                 out=hid_codes[:].bitcast(FP8X4), scales=hid_scales[:], in_=woven[:].rearrange("p j t -> p (j t)")
             )
-            acc = psum.tile([P, part], F32, name="dm%d" % h)
+            acc = psum.tile([P, width], F32, name=bank_name)
             nc.tensor.matmul_mx(
                 out=acc[:],
                 lhsT=w3_codes[:].bitcast(FP8X4),
@@ -288,7 +295,6 @@ def tile_picked_ynewsv_cost_p_kernel(
                 start=True,
                 stop=True,
             )
-            result = work.tile([P, part], F32, name="result")
-            evict = nc.scalar.copy if h == 0 else nc.vector.tensor_copy
-            evict(out=result[:], in_=acc[:])
-            nc.sync.dma_start(out=out[:, cols], in_=result[:])
+            result = work.tile([P, width], F32, name="result")
+            copy(out=result[:], in_=acc[:])
+            nc.sync.dma_start(out=out[:, c0:c1], in_=result[:])

import math
from contextlib import ExitStack

import concourse.mybir as mybir
from concourse.masks import make_identity

K, T, S, N, H = 1024, 2048, 512, 128, 512
FLOPS = 2 * (2 * K * H * S + H * N * S)

F32 = mybir.dt.float32
BF16 = mybir.dt.bfloat16
I32 = mybir.dt.int32
U32 = mybir.dt.uint32
U16 = mybir.dt.uint16
U8 = mybir.dt.uint8
FP8X4 = mybir.dt.float8_e4m3fn_x4
ALU = mybir.AluOpType
ACT = mybir.ActivationFunctionType

P = 128
PACK = 4
K_PASS = P * PACK
PASSES = K // K_PASS
RUN = 4
GROUP = PACK * RUN
PER_COLUMN = 16
CLAMP = 20.0
W1_VECTOR_COLUMNS = 352
WORK_BUFS = 4


def tile_picked_ynewsv_cost_p_kernel(
    tc, x_words, x_scales, w1, w2, pen, unit, w3, offs, nb1, nb2, out
):
    nc = tc.nc
    with ExitStack() as ctx:
        keep = ctx.enter_context(tc.tile_pool(name="keep", bufs=1))
        work = ctx.enter_context(tc.tile_pool(name="work", bufs=WORK_BUFS))
        psum = ctx.enter_context(tc.psum_pool(name="psum", bufs=1))

        def load_list(name, src):
            entries = keep.tile([P, S // PER_COLUMN], U16, name=name)
            nc.sync.dma_start(entries[:], src)
            return entries

        def load_weight(name, w, g, c0, width):
            raw = keep.tile([P, PACK, width], F32, name=name)
            rows = w[g * K_PASS : (g + 1) * K_PASS, c0 : c0 + width]
            nc.sync.dma_start(out=raw[:], in_=rows.rearrange("(p j) c -> p j c", j=PACK))
            return raw

        def load_words(g):
            words = keep.tile([P, T], U32, name="x_words%d" % g)
            nc.sync.dma_start(out=words[:].bitcast(I32), in_=x_words[g].rearrange("p n r -> p (n r)").bitcast(I32))
            return words

        def cast(copy, grouped, raw, c0, width, r0=0):
            dst = grouped[:].rearrange("p (t u q j) -> p u t q j", t=PACK, q=RUN, j=PACK)
            src = raw[:].rearrange("p j (u t q) -> p u t q j", t=PACK, q=RUN)
            copy(out=dst[:, c0 // GROUP : (c0 + width) // GROUP], in_=src[:, r0 // GROUP : (r0 + width) // GROUP])

        def weight_tiles(name):
            grouped = keep.tile([P, PACK * H], BF16, name=name + "_bf16", align_bytes=64)
            codes = keep.tile([P, H], U32, name=name + "_codes", align_bytes=64)
            scales = keep.tile([P, H], U8, name=name + "_scales", align_bytes=64)
            return grouped, codes, scales

        def quantize(tiles, word0, words):
            grouped, codes, scales = tiles
            nc.vector.quantize_mx(
                out=codes[:, word0 : word0 + words].bitcast(FP8X4),
                scales=scales[:, word0 : word0 + words],
                in_=grouped[:, PACK * word0 : PACK * (word0 + words)],
            )

        x_scale_table = keep.tile([P, T], U8, name="x_scale_table")
        nc.vector.memset(x_scale_table[:].bitcast(I32), 0)
        offs_list = load_list("offs_list", offs)
        w1_raw0 = load_weight("w1_raw0", w1, 0, 0, H)
        for quadrant in range(4):
            nc.sync.dma_start(
                out=x_scale_table[32 * quadrant : 32 * quadrant + 4 * PASSES, :].bitcast(I32),
                in_=x_scales[:, 4 * quadrant : 4 * quadrant + 4, :].bitcast(I32),
            )
        x_word_tables = [load_words(g) for g in range(PASSES)]
        factors = keep.tile([P, 2, GROUP], F32, name="factors")
        for n, vec in enumerate((pen, unit)):
            groups = vec.rearrange("(u r) o -> u (r o)", r=GROUP)
            nc.gpsimd.dma_start(out=factors[:, n, :], in_=groups.unsqueeze(1).to_broadcast([P // RUN, RUN, GROUP]))
        w1_raw1 = load_weight("w1_raw1", w1, 1, 0, H)
        w2_raw0 = load_weight("w2_raw0", w2, 0, 0, H)
        last_pieces = ((0, H // 2), (H // 2, H // 2))
        last_piece_names = ["w2_raw1_%d" % c0 for c0, width in last_pieces]
        w2_raw1 = [load_weight(name, w2, 1, c0, width) for name, (c0, width) in zip(last_piece_names, last_pieces)]
        nb1_list = load_list("nb1_list", nb1)
        nb2_list = load_list("nb2_list", nb2)
        w3_raw = keep.tile([P, PACK, N], F32, name="w3_raw")
        w3_rows = w3.rearrange("(u t q) m -> t u q m", t=PACK, q=RUN)
        for t in range(PACK):
            nc.sync.dma_start(out=w3_raw[:, t, :], in_=w3_rows[t])

        identity = keep.tile([P, P], F32, name="identity")
        make_identity(nc, identity[:])
        own = keep.tile([P, RUN], F32, name="own")
        nc.vector.tensor_reduce(own[:], identity[:].rearrange("p (u q) -> p q u", q=RUN), mybir.AxisListType.X, ALU.add)
        masked = keep.tile([P, 2 * PACK, RUN], F32, name="masked")
        nc.gpsimd.tensor_tensor(
            masked[:],
            factors[:].rearrange("p n (t q) -> p (n t) q", q=RUN),
            own[:].unsqueeze(1).to_broadcast([P, 2 * PACK, RUN]),
            ALU.mult,
        )
        pairs = keep.tile([P, 2 * PACK, 2], F32, name="pairs")
        nc.gpsimd.tensor_tensor(pairs[:], masked[:, :, 0:2], masked[:, :, 2:4], ALU.add)
        picked = keep.tile([P, 2 * PACK], F32, name="picked")
        nc.gpsimd.tensor_tensor(picked[:], pairs[:, :, 0], pairs[:, :, 1], ALU.add)
        pen_own = picked[:, 0:PACK]
        unit_own = picked[:, PACK : 2 * PACK]
        sign = keep.tile([P, PACK], BF16, name="sign")
        step = keep.tile([P, PACK], F32, name="step")
        size = keep.tile([P, PACK], F32, name="size")
        gain = keep.tile([P, PACK], F32, name="gain")
        neg_gain = keep.tile([P, PACK], F32, name="neg_gain")
        neg_size = keep.tile([P, PACK], F32, name="neg_size")
        slope = keep.tile([P, PACK], F32, name="slope")
        share = keep.tile([P, PACK], F32, name="share")
        nc.gpsimd.tensor_scalar(step[:], unit_own, 0.0, 2.0, ALU.is_ge, ALU.mult)
        nc.gpsimd.tensor_scalar(sign[:], step[:], 1.0, -1.0, ALU.mult, ALU.add)
        nc.gpsimd.tensor_tensor(size[:], unit_own, sign[:], ALU.mult)
        nc.gpsimd.tensor_scalar(gain[:], size[:], 0.8, 0.0, ALU.mult, ALU.add)
        nc.gpsimd.tensor_scalar(neg_gain[:], size[:], -0.8, 0.0, ALU.mult, ALU.add)
        nc.gpsimd.tensor_scalar(neg_size[:], size[:], -1.0, 0.0, ALU.mult, ALU.add)
        nc.gpsimd.tensor_tensor(slope[:], neg_size[:], pen_own, ALU.mult)
        nc.gpsimd.tensor_scalar(share[:], pen_own, -1.25, 0.625, ALU.mult, ALU.add)

        x_scale_rows = keep.tile([P, S], U8, name="x_scale_rows", align_bytes=64)
        nc.vector.tensor_copy(x_scale_rows[:], x_scale_table[:].indirect(offs_list[:]))
        x_codes = [keep.tile([P, S], U32, name="x_codes%d" % g, align_bytes=64) for g in range(PASSES)]

        def product(bank, tiles, g, t):
            grouped, codes, scales = tiles
            nc.tensor.matmul_mx(
                out=bank[:],
                lhsT=codes[:, t * P : (t + 1) * P].bitcast(FP8X4),
                lhsT_scale=scales[:, t * P : (t + 1) * P],
                rhs=x_codes[g][:].bitcast(FP8X4),
                rhs_scale=x_scale_rows[4 * g : P, :],
                start=(g == 0),
                stop=(g == PASSES - 1),
            )

        w1_mx = [weight_tiles("w1_%d" % g) for g in range(PASSES)]
        w2_mx = [weight_tiles("w2_%d" % g) for g in range(PASSES)]
        dm_names = ["dm%d" % t for t in range(PACK)]
        dm = [psum.tile([P, S], F32, name=name) for name in dm_names]
        st = [psum.tile([P, S], F32, name="st%d" % t) for t in range(PACK)]

        cast(nc.scalar.copy, w1_mx[0][0], w1_raw0, 0, H)
        nc.vector.tensor_copy(x_codes[0][:], x_word_tables[0][:].indirect(offs_list[:]))
        quantize(w1_mx[0], 0, H)
        for t in range(PACK):
            product(dm[t], w1_mx[0], 0, t)
        nc.vector.tensor_copy(x_codes[1][:], x_word_tables[1][:].indirect(offs_list[:]))
        cast(nc.vector.tensor_copy, w1_mx[1][0], w1_raw1, 0, W1_VECTOR_COLUMNS)
        cast(nc.scalar.copy, w1_mx[1][0], w1_raw1, W1_VECTOR_COLUMNS, H - W1_VECTOR_COLUMNS, W1_VECTOR_COLUMNS)
        for t in range(PACK):
            quantize(w1_mx[1], t * P, P)
            product(dm[t], w1_mx[1], 1, t)

        exp_dm = [keep.tile([P, S], F32, name="exp_dm%d" % t) for t in range(PACK)]
        for t in range(PACK):
            nc.scalar.activation(exp_dm[t][:], dm[t][:], ACT.Exp)
        cast(nc.vector.tensor_copy, w2_mx[0][0], w2_raw0, 0, H)
        quantize(w2_mx[0], 0, H)
        for t in range(PACK):
            product(st[t], w2_mx[0], 0, t)
        for raw, (c0, width) in zip(w2_raw1, last_pieces):
            cast(nc.vector.tensor_copy, w2_mx[1][0], raw, c0, width)
        for t in range(PACK):
            quantize(w2_mx[1], t * P, P)
            product(st[t], w2_mx[1], 1, t)

        one_plus = keep.tile([P, PACK * S], F32, name=last_piece_names[-1])
        for t in range(PACK):
            nc.vector.tensor_scalar(one_plus[:, t * S : (t + 1) * S], exp_dm[t][:], math.exp(CLAMP), 1.0, ALU.min, ALU.add)
        ratio = [keep.tile([P, S], F32, name="ratio%d" % t) for t in range(PACK)]
        for t in range(PACK):
            nc.scalar.activation(ratio[t][:], st[t][:], ACT.Sigmoid, scale=-1.0)
        for t in range(PACK):
            nc.vector.scalar_tensor_tensor(
                ratio[t][:], ratio[t][:], 1.0 / (1.0 + math.exp(CLAMP)), one_plus[:, t * S : (t + 1) * S], ALU.max, ALU.mult
            )

        w3_bf16 = keep.tile([P, N, PACK], BF16, name="w3_bf16", align_bytes=64)
        w3_codes = keep.tile([P, N], U32, name="w3_codes", align_bytes=64)
        w3_scales = keep.tile([P, N], U8, name="w3_scales", align_bytes=64)
        w3_woven = keep.tile([P, N, PACK], BF16, name="w3_woven")
        nc.vector.tensor_copy(w3_woven[:], w3_raw[:].rearrange("p t m -> p m t"))
        nc.vector.tensor_tensor(w3_bf16[:], w3_woven[:], sign[:].unsqueeze(1).to_broadcast([P, N, PACK]), ALU.mult)
        nc.vector.quantize_mx(
            out=w3_codes[:].bitcast(FP8X4), scales=w3_scales[:], in_=w3_bf16[:].rearrange("p m t -> p (m t)")
        )

        hid = keep.tile([P, PACK, S], BF16, name="hid")
        windows = [keep.tile([P, 2 * S], F32, name="window%d" % t) for t in range(PACK)]
        lifted = [keep.tile([P, S], F32, name="lifted%d" % t) for t in range(PACK)]
        first = {t: keep.tile([P, S], F32, name="first%d" % t) for t in range(1, PACK, 2)}
        second = [keep.tile([P, S], F32, name="second%d" % t) for t in range(PACK)]
        base = [keep.tile([P, S], F32, name="base%d" % t) for t in range(PACK)]
        offer = [keep.tile([P, S], F32, name="offer%d" % t) for t in range(PACK)]
        moved = [keep.tile([P, S], F32, name="moved%d" % t) for t in range(PACK)]

        def lift(t):
            log_ratio = work.tile([P, S], F32, name="log_ratio")
            nc.scalar.activation(log_ratio[:], ratio[t][:], ACT.Ln)
            nc.vector.scalar_tensor_tensor(lifted[t][:], dm[t][:], CLAMP, log_ratio[:], ALU.max, ALU.add)

        def net_of(t):
            nc.vector.scalar_tensor_tensor(windows[t][:, S:], st[t][:], CLAMP, lifted[t][:], ALU.max, ALU.subtract)

        def surplus_of(t):
            nc.scalar.activation(windows[t][:, :S], windows[t][:, S:], ACT.Relu, scale=gain[:, t : t + 1])

        def fetch(t, c0, c1):
            entries = slice(c0 // PER_COLUMN, c1 // PER_COLUMN)
            nc.scalar.activation(second[t][:, c0:c1], windows[t][:].indirect(nb2_list[:, entries]), ACT.Copy, scale=0.5)
            if t in first:
                nc.scalar.activation(first[t][:, c0:c1], windows[t][:].indirect(nb1_list[:, entries]), ACT.Copy)

        def base_of(t):
            nc.vector.scalar_tensor_tensor(
                base[t][:], windows[t][:, S:], slope[:, t : t + 1], windows[t][:, :S], ALU.mult, ALU.add
            )

        def offer_of(t, c0, c1):
            entries = slice(c0 // PER_COLUMN, c1 // PER_COLUMN)
            source = first[t][:, c0:c1] if t in first else windows[t][:].indirect(nb1_list[:, entries])
            nc.vector.tensor_tensor(offer[t][:, c0:c1], source, second[t][:, c0:c1], ALU.add)

        def moved_of(t, c0, c1):
            net = windows[t][:, S + c0 : S + c1]
            nc.vector.scalar_tensor_tensor(
                moved[t][:, c0:c1], net, neg_gain[:, t : t + 1], offer[t][:, c0:c1], ALU.mult, ALU.min
            )

        def hid_of(t, c0, c1):
            nc.vector.scalar_tensor_tensor(
                hid[:, t, c0:c1], moved[t][:, c0:c1], share[:, t : t + 1], base[t][:, c0:c1], ALU.mult, ALU.add
            )

        last = PACK - 1
        lift(0)
        for t in range(PACK):
            if t < last:
                lift(t + 1)
            net_of(t)
        surplus_of(0)
        base_of(0)
        for t in range(last):
            fetch(t, 0, S)
            surplus_of(t + 1)
            offer_of(t, 0, S)
            if t > 0:
                hid_of(t - 1, 0, S)
            base_of(t + 1)
            moved_of(t, 0, S)
        halves = ((0, S // 2), (S // 2, S))
        for c0, c1 in halves:
            fetch(last, c0, c1)
        offer_of(last, *halves[0])
        hid_of(last - 1, *halves[0])
        moved_of(last, *halves[0])
        offer_of(last, *halves[1])
        hid_of(last, *halves[0])
        moved_of(last, *halves[1])
        hid_of(last - 1, *halves[1])
        hid_of(last, *halves[1])

        for (c0, c1), copy, bank_name in zip(halves, (nc.scalar.copy, nc.vector.tensor_copy), dm_names):
            width = c1 - c0
            woven = work.tile([P, width, PACK], BF16, name="woven", align_bytes=64)
            copy(out=woven[:], in_=hid[:, :, c0:c1].rearrange("p t j -> p j t"))
            hid_codes = work.tile([P, width], U32, name="hid_codes", align_bytes=64)
            hid_scales = work.tile([P, width], U8, name="hid_scales", align_bytes=64)
            nc.vector.quantize_mx(
                out=hid_codes[:].bitcast(FP8X4), scales=hid_scales[:], in_=woven[:].rearrange("p j t -> p (j t)")
            )
            acc = psum.tile([P, width], F32, name=bank_name)
            nc.tensor.matmul_mx(
                out=acc[:],
                lhsT=w3_codes[:].bitcast(FP8X4),
                lhsT_scale=w3_scales[:],
                rhs=hid_codes[:].bitcast(FP8X4),
                rhs_scale=hid_scales[:],
                start=True,
                stop=True,
            )
            result = work.tile([P, width], F32, name="result")
            copy(out=result[:], in_=acc[:])
            nc.sync.dma_start(out=out[:, c0:c1], in_=result[:])
